import numpy as np, ml_dtypes
CORES = [6,15,38,47]
N = 4
import mx_ref
BF = ml_dtypes.bfloat16
def gcols(t, e):
    v = np.concatenate([t.reshape(8, 16, -1, 4), np.zeros((8, 16, 1, 4), BF)], axis=2)
    return np.ascontiguousarray(np.stack([v[g][:, e[g]] for g in range(8)])).reshape(128, -1)
def tile(rs):
    return np.stack(rs, axis=2).reshape(128, -1).astype(BF)
def cut(t, i, w=512):
    return t[:, w * i:w * i + w]
def pick(q, e):
    c = np.concatenate([q[0].reshape(128, -1, 4), np.zeros((128, 1, 4), np.uint8)], axis=1); s = np.concatenate([q[1], np.ones((16, 1), np.uint8)], axis=1)
    return (np.ascontiguousarray(c[:, e].reshape(128, -1)), np.ascontiguousarray(s[:, e]))
def join(*qs):
    return (np.concatenate([q[0] for q in qs], axis=1), np.concatenate([q[1] for q in qs], axis=1))
def put(q, e, v):
    c, s = q[0].reshape(128, -1, 4).copy(), q[1].copy(); c[:, e] = v[0].reshape(128, -1, 4); s[:, e] = v[1]
    return (c.reshape(128, -1), s)
def pk(c, s):
    return (np.ascontiguousarray(c), mx_ref.live(s))
def emit(q):
    return q[0], q[1]
def packed(v, rng):
    q = [mx_ref.quantize(np.ascontiguousarray(v[r])) for r in range(N)]
    return np.stack([a for a, b in q]), np.stack([mx_ref.plane(b, rng) for a, b in q])
def values_of_codes():
    e, c = np.zeros((128, 128, 4), np.float32), np.zeros((128, 2, 4), np.uint8)
    e[np.arange(128), np.arange(128), 0] = 1
    c[:127, :, 0] = np.arange(256).reshape(2, 128).T[:127]
    return mx_ref.matmul(mx_ref.quantize(e.reshape(128, 512).astype(BF)), (c.reshape(128, 8), np.full((16, 2), 127, np.uint8))).T.reshape(-1).astype(np.float64)
CODE_VALUE, SCALE_VALUE = values_of_codes(), 2.0 ** (np.arange(256) - 127.0)
def decode(q):
    return (CODE_VALUE[q[0]].reshape(16, 8, -1, 4) * SCALE_VALUE[q[1]][:, None, :, None] + 0.0).reshape(128, -1).astype(np.float32)
def f(rng, *shape):
    return mx_ref.flush((rng.standard_normal(shape, dtype=np.float32) * np.exp2(rng.integers(-2, 3, shape[:-1] + (1,)))).astype(BF))
def wide(rng, *shape, cols=0):
    v = rng.standard_normal(shape, dtype=np.float32) * np.exp2(rng.integers(-12, 13, shape)).astype(np.float32)
    if cols: v *= np.repeat(np.exp2(rng.integers(-cols, cols + 1, shape[:-2] + (1, shape[-1] // 4))) * (rng.random(shape[:-2] + (1, shape[-1] // 4)) > 0.0625), 4, axis=-1).astype(np.float32)
    return mx_ref.flush(v.astype(BF))
C, H, R, STEP = 448, 128, 3, 13
def big(v):
    v = v.astype(np.float32)
    v[np.abs(v) < np.float32(2.0 ** -16)] = 0
    return v.astype(BF)
def numbers_of(rng):
    return {"x": big(f(rng, N, 128, 4 * C)), "u": np.array(f(rng, N, 128, 512)), "v": np.array(f(rng, N, 128, 512))}
def plays(rng):
    return rng.integers(1, 7, (N, 8, 1)).astype(np.int32)
def layers(rng):
    return big(f(rng, N, 128, 2048)).reshape(N, 8, 16, 4, 8, 16, 4)
def weights(rng, w):
    c, s = packed(np.ascontiguousarray(w).reshape(N, 128, 2048), rng)
    return {"wc": c, "ws": s}
def turning(rng):
    b = np.abs(128 - (STEP * np.arange(130)) % 256)
    k = np.flatnonzero((b[1:129] - b[:128]) * (b[2:] - b[1:129]) < 0) + 1
    e = min(STEP, C // 32) - 1
    k = np.concatenate([[0], k[:e], [128]])
    s = -np.ones(C)
    for i in range(e + 1):
        lo = 32 * i
        hi = lo + 32 if i < e else C
        m = [lo, hi - 1]
        w = rng.permutation(np.setdiff1d(np.arange(lo, hi), m))
        s[m] = 1
        s[w[:k[i + 1] - k[i] - len(m)]] = 1
    return s
def setup_inputs(rng):
    return {**numbers_of(rng), "p": plays(rng), **weights(rng, layers(rng))}
def setup_inputs_ties(rng):
    d = numbers_of(rng)
    e = rng.permutation(N)
    x = d["x"].reshape(N, 8, 16, C, 4)
    a = (1.0 + (2 * rng.integers(0, 64, (N, 8, 8, C, 4)) + 1) * 2.0 ** -7) * np.exp2(-rng.integers(8, 15, (N, 8, 8, C, 4)).astype(np.float64))
    a *= rng.integers(0, 2, a.shape) * 2.0 - 1.0
    a[:, :, 0, :, 0] = 1.96875
    x[:, :, 8:] = a.astype(np.float32).astype(BF)
    for r in range(N):
        k = rng.permutation(C) % 3
        if r == e[0]: k = np.ones(C, int)
        elif r in e[2::2]: k = rng.permutation(3)[np.arange(C) % 3]
        c = x[r, 0, :8, :3].copy()
        c[:, 0] = 0
        c[:, 2] = -c[:, 1]
        x[r, 0, :8] = c[:, k]
    x[e[1]] = 0
    u = d["u"].reshape(N, 8, 16, 128, 4)
    u[:, 1:, :, 0] = 0
    u[:, 0, 8:, 0] = 0
    w = layers(rng)
    w[:, :, :, :, 0, :8] = 0
    return {"x": x.reshape(N, 128, 4 * C), "u": u.reshape(N, 128, 512), "v": d["v"], "p": plays(rng), **weights(rng, w)}
def setup_inputs_near(rng):
    d = numbers_of(rng)
    x = d["x"].reshape(N, 8, 16, C, 4)
    u = d["u"].reshape(N, 128, 128, 4)
    o = rng.permutation(N) % 2
    x[:, 0, 0] = 0
    x[:, 0, 8:] = 0
    u[:, :, 0] = 0
    for r in range(N):
        k = 2.0 ** -30 if o[r] == 0 else 1.0
        c = rng.permutation(C) % 3
        x[r, 0, 8, :, 0] = (np.array([9, 8, 9])[c] * 0.125 * k).astype(np.float32).astype(BF)
        x[r, 0, 9, :, 0] = (np.array([10, 9, 11])[c] * 0.125 * k).astype(np.float32).astype(BF)
        x[r, 0, 0, rng.integers(C), 0] = 2.0 ** 29 * (rng.integers(0, 2) * 2.0 - 1.0)
        u[r, 0, 0, 0] = k
        u[r, 8, 0, 0] = 1.125 * k
        u[r, 9, 0, 0] = -k
    w = layers(rng)
    for i in [0] + [8 + j for j in range(8)]:
        w[:, 0, i] = 0
        w[:, :, :, :, 0, i] = 0
    return {"x": x.reshape(N, 128, 4 * C), "u": u.reshape(N, 128, 512), "v": d["v"], "p": plays(rng), **weights(rng, w)}
def setup_inputs_late(rng):
    d = numbers_of(rng)
    x = d["x"].reshape(N, 128, C, 4)
    k = rng.permutation(N) % 2
    c = (k * 2.0 - 1.0).astype(np.float32).astype(BF)
    x[:, 0] = c[:, None, None]
    x[:, 1:8] = np.clip(x[:, 1:8].astype(np.float32), -8, 8).astype(BF)
    u = d["u"].reshape(N, 128, 128, 4)
    u[:, :, 0] = 0
    u[:, 0, 0, 0] = 1
    p = plays(rng)
    p[k == 0, 0] = 1
    p[np.flatnonzero(k == 1)[0]] = 6
    return {"x": x.reshape(N, 128, 4 * C), "u": u.reshape(N, 128, 512), "v": d["v"], "p": p, **weights(rng, layers(rng))}
def setup_inputs_ends(rng):
    d = numbers_of(rng)
    x = np.zeros((N, 8, 16, C, 4), np.float32)
    u = d["u"].reshape(N, 128, 128, 4)
    v = d["v"]
    o = rng.permutation(N) % 4
    for t in range(N):
        for r in range(N):
            if o[r] == 3 and o[(r + 1) % N] == 2:
                o[r] = 2
                o[(r + 1) % N] = 3
    h = rng.permutation(N) % 2
    m = np.flatnonzero(o == 1)
    if (h[m] == 0).all():
        h[np.flatnonzero(h == 1)[0]] = 0
        h[m[0]] = 1
    p = np.zeros((N, 8, 1), np.int32)
    w = np.zeros((N, 128, 4, 128, 4), np.float32)
    i = np.arange(128)
    u[:, :, 0] = 0
    for r in range(N):
        p[r] = 6 if h[r] == 0 else 1
        for b in range(4): w[r, i, b, i, b] = 1 if o[r] == 3 else -1
        if o[r] < 3:
            a = rng.integers(8, 17, (8, 1, C, 1)) * 2.0 ** 26
            x[r] = a if o[r] == 0 else -a if o[r] == 1 else a * turning(rng)[None, None, :, None]
            u[r, :, 0] = 2.0 ** 30
        else:
            x[r] = rng.integers(8, 16, (8, 1, C, 1)) * 2.0 ** -33
            x[r, 0, 0, :, 0] = (2 + rng.permutation(C) % 3) * 2.0 ** -31
            x[r, 0, 1, :, 0] = 2.0 ** -30
            u[r, 0, 0, 0] = 2.0 ** -30
            u[r, 1, 0, 0] = -1.5 * 2.0 ** -30
        if o[r] in (0, 2): v[r] = (2.0 ** 30 * (rng.integers(0, 2, (128, 512)) * 2.0 - 1.0)).astype(np.float32).astype(BF)
        if o[r] == 3: v[r] = 2.0 ** -30
    return {"x": x.reshape(N, 128, 4 * C).astype(BF), "u": u.reshape(N, 128, 512), "v": v, "p": p, **weights(rng, w.astype(BF))}
def setup_inputs_spread(rng):
    d = setup_inputs(rng)
    d["x"] = big(wide(rng, N, 128, 4 * C, cols=6))
    return d
def check_inputs(d):
    b = []
    for k in ("x", "u", "v"):
        a = np.abs(d[k].astype(np.float32))
        if not (np.isfinite(a).all() and ((a == 0) | (a >= 2.0 ** -30) & (a <= 2.0 ** 30)).all()): b.append("a value of " + k)
    if not ((d["p"] >= 1) & (d["p"] <= 6)).all(): b.append("an entry of p")
    none, least, most = [emit(mx_ref.quantize(np.full((128, 16), k, np.float32).astype(BF)))[1][0, 0] for k in (0.0, 2.0 ** -30, 2.0 ** 30)]
    for r in range(N):
        if ((d["wc"][r] == 0x7F) | (d["wc"][r] == 0xFF)).any(): b.append("wc: a code that is no number")
        s = mx_ref.live(d["ws"][r])
        if ((s != none) & ((s < least) | (s > most))).any(): b.append("ws: a scale out of range")
    return b
def reference(x, u, v, p, wc, ws):
    qu = [mx_ref.quantize(u[r]) for r in range(N)]
    lay = [pk(wc[r], ws[r]) for r in range(N)]
    now = [x[r] for r in range(N)]
    n, kept = np.zeros(N, np.int64), np.zeros((N, 8), np.int64)
    a = np.zeros((N, 8, C), np.int64)
    for t in range(R):
        q = [mx_ref.quantize(now[r]) for r in range(N)]
        held = [decode(q[r]).astype(BF) for r in range(N)]
        s = np.stack([mx_ref.matmul(qu[r], q[r])[0] > 0 for r in range(N)])
        for j in range(C):
            n = n + s[:, j]
            c = np.abs(128 - (STEP * n) % 256)
            for g in range(8):
                c = np.minimum(np.maximum(kept[:, g], c - p[:, g, 0]), c + p[:, g, 0])
                kept[:, g] = c
            a[:, :, j] = kept
        made = []
        for r in range(N):
            window = np.concatenate([held[r], cut(held[(r + 1) % N], 0, 4 * H)], axis=1)
            far = gcols(window, np.arange(C) + a[r])
            z = mx_ref.quantize(((held[r].astype(np.float32) + far.astype(np.float32)) * np.float32(0.5)).astype(BF))
            made.append(tile([mx_ref.matmul(pick(lay[r], np.arange(128 * b, 128 * b + 128)), z) * np.float32(0.03125) + now[r][:, b::4].astype(np.float32) for b in range(4)]))
        now = made
    y, ao = np.zeros((N, 128, C), np.float32), np.zeros((N, 8, C), np.float32)
    oc, osc = np.zeros((N, 128, 4 * C), np.uint8), np.zeros((N, 16, C), np.uint8)
    for r in range(N):
        q = mx_ref.quantize(now[r])
        y[r] = mx_ref.matmul(mx_ref.quantize(v[r]), q)
        ao[r] = a[r]
        oc[r], osc[r] = emit(q)
    return {"y": y, "ao": ao, "oc": oc, "osc": osc}

from concourse.mybir import dt, AluOpType, AxisListType, ActivationFunctionType

C, H, R, STEP = 448, 128, 3, 13
C1 = 320
LC = C // 16
MW = 2 * LC + 4
NM = 158
BIG = 1.0e29
BIG2 = 1.0e28
ZAT = 2
NEARLY = 1
GRP = (0, 128, 192, 320)
CAST1 = "svsv"
CAST2 = "ssss"
NENG = 8

F8, U8, BF, F32, I32, U16 = "float8_e4m3fn_x4", "uint8", "bfloat16", "float32", "int32", "uint16"
SCRATCH = {
    "xt": ("sbuf", [128, 4 * C], BF), "yt": ("sbuf", [128, 4 * C], BF), "zt": ("sbuf", [128, 4 * C], BF),
    "ut": ("sbuf", [128, 512], BF), "vt": ("sbuf", [128, 512], BF),
    "qu": ("sbuf", [128, 128], F8), "su": ("sbuf", [128, 128], U8),
    "qv": ("sbuf", [128, 128], F8), "sv": ("sbuf", [128, 128], U8),
    "qw": ("sbuf", [128, 512], F8), "sw": ("sbuf", [128, 512], U8),
    "qe": ("sbuf", [128, 512], F8), "se": ("sbuf", [128, 512], U8),
    "qee": ("sbuf", [128, 512], F8), "see": ("sbuf", [128, 512], U8),
    "qeo": ("sbuf", [128, 512], F8), "seo": ("sbuf", [128, 512], U8),
    "ql": ("sbuf", [128, 256], F8), "sl": ("sbuf", [128, 256], U8),
    "ebuf": ("sbuf", [128, 520], BF), "ebe": ("sbuf", [128, 520], BF), "ebo": ("sbuf", [128, 520], BF),
    "ones": ("sbuf", [128, 512], BF), "lio": ("sbuf", [128, 512], BF), "ltri": ("sbuf", [128, 512], BF),
    "mt": ("sbuf", [128, 4 * NM], BF),
    "thr": ("sbuf", [128, 4 * MW], F32), "dd": ("sbuf", [128, 4 * LC], F32), "lo": ("sbuf", [128, 4 * LC], F32), "hi": ("sbuf", [128, 4 * LC], F32),
    "pi": ("sbuf", [128, 4], I32), "pm": ("sbuf", [128, 4], I32), "pb": ("sbuf", [128, 4], I32), "pf": ("sbuf", [128, 4], F32), "ipf": ("sbuf", [128, 4], F32),
    "ge": ("sbuf", [128, 4], F32), "go": ("sbuf", [128, 4], F32),
    "prow": ("sbuf", [1, 8], I32), "prf": ("sbuf", [1, 10], F32), "pall": ("sbuf", [128, 10], F32), "pme": ("sbuf", [128, 10], F32), "pmo": ("sbuf", [128, 8], F32),
    "jio": ("sbuf", [128, 2 * LC], F32), "jt": ("sbuf", [128, 2 * LC], F32), "atab": ("sbuf", [128, 128], F32),
    "fz": ("sbuf", [128, 4], F32),
    "hh": ("sbuf", [128, LC], I32), "rr": ("sbuf", [128, LC], I32), "par": ("sbuf", [128, LC], I32), "sg": ("sbuf", [128, LC], F32),
    "vv": ("sbuf", [128, LC], F32), "nv": ("sbuf", [128, LC], F32), "xx": ("sbuf", [128, LC], F32), "nx": ("sbuf", [128, LC], F32), "z1": ("sbuf", [128, LC], F32),
    "sy": ("sbuf", [128, 2 * LC], F32), "of": ("sbuf", [128, 2 * LC], F32),
    "a1": ("sbuf", [128, LC], F32), "a2": ("sbuf", [128, LC], F32), "aoff": ("sbuf", [128, LC], U16), "a3": ("sbuf", [128, LC], F32),
    "ag": ("sbuf", [128, C], F32), "yo": ("sbuf", [128, C], F32),
    "ps": ("psum", [128, 4096], F32),
}
for _k in "eo":
    for _n in ("pc", "pz", "t1", "t2", "yy"):
        SCRATCH[_n + _k] = ("sbuf", [128, LC], F32)
for _t in range(R):
    for _n, _w, _d in (("off", 2 * LC, U16), ("qz", C, F8), ("sz", C, U8), ("qm", NM, F8), ("sm", NM, U8), ("base", 4, F32), ("hb", 4, F32),
                       ("nce", 4, F32), ("nco", 4, F32), ("qfe", C, F8), ("sfe", C, U8), ("qfo", C, F8), ("sfo", C, U8)):
        SCRATCH["%s%d" % (_n, _t)] = ("sbuf", [128, _w], _d)
for _t in range(R + 1):
    SCRATCH["qx%d" % _t] = ("sbuf", [128, C + H], F8)
    SCRATCH["sx%d" % _t] = ("sbuf", [128, C + H], U8)
NDMA = 28
SEMAPHORES = ["qv_", "qs_", "qp_", "qg_", "loc"] + ["arr%d" % t for t in range(R)] + ["d%d" % k for k in range(NDMA)]


def rank_program(g, core, T, topo):
    rank = T.rank_of(core)
    if rank is None:
        return
    A = AluOpType
    ACT = ActivationFunctionType
    Q = {"v": g.vector, "s": g.scalar, "p": g.tensor, "g": g, "y": g.sync}
    cnt = {"v": 0, "s": 0, "p": 0, "g": 0}
    know = {k: {} for k in Q}
    log = {}
    ndma = [0]
    tot = {}
    seq = [0]

    def reg(name, lo, hi, step=1):
        return (name, lo, hi, step, lo % step)

    def await_(q, tok):
        sem, val, snap = tok
        k = know[q]
        if k.get(sem, 0) < val:
            Q[q].wait_ge(T.sem[sem], val)
            k[sem] = val
        for s, n in snap.items():
            if k.get(s, 0) < n:
                k[s] = n

    def deps(q, rd, wr, acc=False):
        out = []
        for acs, w in ((rd, False), (wr, True)):
            for (nm, lo, hi, st, ph) in acs:
                for (l2, h2, s2, p2, w2, q2, tok, order) in log.get(nm, ()):
                    if nm == "ps":
                        if lo // 512 != l2 // 512: continue
                        if q2 == q and not w and not w2: continue
                    else:
                        if hi <= l2 or h2 <= lo: continue
                        if st == s2 and st > 1 and ph != p2: continue
                        if not w and not w2: continue
                    if q2 == q and tok[0][0] == "q":
                        if w and not w2: continue
                        if acc and w and w2: continue
                    out.append((order, tok))
        out.sort(key=lambda a: -a[0])
        return [a[1] for a in out]

    def note(q, rd, wr, tok):
        seq[0] += 1
        for acs, w in ((rd, False), (wr, True)):
            for (nm, lo, hi, st, ph) in acs:
                L = log.setdefault(nm, [])
                if w and nm == "ps":
                    L[:] = [e for e in L if e[0] // 512 != lo // 512]
                elif w:
                    L[:] = [e for e in L if not (lo <= e[0] and e[1] <= hi and (st == 1 or (st == e[2] and ph == e[3])))]
                L.append((lo, hi, st, ph, w, q, tok, seq[0]))

    def ins(q, fn, rd, wr, acc=False):
        for d in deps(q, rd, wr, acc):
            await_(q, d)
        sem = "q%s_" % q
        cnt[q] += 1
        fn().then_inc(T.sem[sem], 1)
        snap = dict(know[q])
        snap[sem] = cnt[q]
        tot[sem] = cnt[q]
        note(q, rd, wr, (sem, cnt[q], snap))

    def dma(q, out, in_, rd, wr):
        for d in deps(q, rd, wr):
            await_(q, d)
        sem = "d%d" % ndma[0]
        ndma[0] += 1
        Q[q].dma_start(out, in_).then_inc(T.sem[sem], 16)
        tot[sem] = 16
        note(q, rd, wr, (sem, 16, dict(know[q])))

    def ap(r):
        nm, lo, hi, st, ph = r
        return T[nm][:, lo:hi] if st == 1 else T[nm][:, lo:hi:st]

    def tt(o, a, b, op):
        ins("v", lambda: g.vector.tensor_tensor(ap(o), ap(a), ap(b), op), [a, b], [o])

    def ts(o, a, s1, s2, op0, op1=None):
        rd = [a] + [s for s in (s1, s2) if isinstance(s, tuple)]
        s1 = ap(s1) if isinstance(s1, tuple) else s1
        s2 = ap(s2) if isinstance(s2, tuple) else s2
        if op1 is None:
            ins("v", lambda: g.vector.tensor_scalar(ap(o), ap(a), s1, None, op0), rd, [o])
        else:
            ins("v", lambda: g.vector.tensor_scalar(ap(o), ap(a), s1, s2, op0, op1), rd, [o])

    def cp(o, a):
        ins("v", lambda: g.vector.tensor_copy(ap(o), ap(a)), [a], [o])

    def fill(o, k):
        ins("v", lambda: g.vector.memset(ap(o), k), [], [o])

    def act(o, a, scale=1.0):
        rd = [a] + ([scale] if isinstance(scale, tuple) else [])
        scale = ap(scale) if isinstance(scale, tuple) else scale
        ins("s", lambda: g.scalar.activation(ap(o), ap(a), ACT.Copy, scale=scale), rd, [o])

    def relu(o, a, f, scale, bias):
        ins("s", lambda: g.scalar.activation(ap(o), ap(a), f, bias=bias, scale=scale), [a], [o])

    def quant(qn, sn, c0, c1, src, e0, e1):
        ins("v", lambda: g.vector.quantize_mx(T[qn][:, c0:c1], T[sn][:, c0:c1], T[src][:, e0:e1]), [reg(src, e0, e1)], [reg(qn, c0, c1), reg(sn, c0, c1)])

    def mm(k, ln, lsn, l0, rn, rsn, r0, r1, start=True, stop=True):
        o = reg("ps", 512 * k, 512 * k + r1 - r0)
        rd = [reg(ln, l0, l0 + 128), reg(lsn, l0, l0 + 128), reg(rn, r0, r1), reg(rsn, r0, r1)]
        ins("p", lambda: g.tensor.matmul_mx(ap(o), T[ln][:, l0:l0 + 128], T[lsn][:, l0:l0 + 128], T[rn][:, r0:r1], T[rsn][:, r0:r1], start, stop), rd, [o], acc=not start)

    def iota(nm, n, pattern, base, cm):
        if SCRATCH[nm][2] == I32:
            ins("g", lambda: g.iota(T[nm][:, 0:n], pattern, base, cm), [], [reg(nm, 0, n)])
        else:
            ins("g", lambda: g.iota(T[nm][:, 0:n], pattern, base, cm, allow_small_or_imprecise_dtypes=True), [], [reg(nm, 0, n)])

    def sel(o, i, pattern, op, fil, base, cm):
        ins("g", lambda: g.affine_select(ap(o), ap(i), pattern, op, fil, base, cm), [i], [o])

    def col(n, c=0):
        return reg(n, c, c + 1)

    def bank(k, n):
        return reg("ps", 512 * k, 512 * k + n)

    P0, P1 = H, C1
    dma("y", T.xt[:, 0:4 * P0], T.x[:, 0:4 * P0], [], [reg("xt", 0, 4 * P0)])
    dma("s", T.prow[0:1, 0:8], T.p[:, :], [], [reg("prow", 0, 8)])
    dma("s", T.ut[:, :], T.u[:, :], [], [reg("ut", 0, 512)])
    dma("y", T.xt[:, 4 * P0:4 * P1], T.x[:, 4 * P0:4 * P1], [], [reg("xt", 4 * P0, 4 * P1)])
    dma("s", T.xt[:, 4 * P1:4 * C], T.x[:, 4 * P1:4 * C], [], [reg("xt", 4 * P1, 4 * C)])
    dma("y", T.qw[:, :].bitcast(dt.uint8), T.wc[:, :], [], [reg("qw", 0, 512)])
    dma("s", T.sw[:, :], T.ws[:, :], [], [reg("sw", 0, 512)])
    dma("y", T.vt[:, :], T.v[:, :], [], [reg("vt", 0, 512)])

    iota("pi", 1, [[0, 1]], 0, 1)
    fill(reg("ones", 0, 512), 1.0)
    fill(reg("ebuf", 0, 520), 0.0)
    sel(reg("ebuf", 4, 516, 4), reg("ones", 0, 128), [[-1, 128]], A.is_equal, 0.0, 0, 1)
    for t in range(4):
        ins("g", lambda: g.iota(T.dd[:, LC * t:LC * t + LC], [[-16, LC]], GRP[t], 1, allow_small_or_imprecise_dtypes=True), [], [reg("dd", LC * t, LC * t + LC)])
    iota("lio", 512, [[0, 8], [1, 16], [0, 4]], 0, 0)
    ts(col("pb"), col("pi"), 16, None, A.bitwise_and)
    ts(col("pm"), col("pi"), 15, None, A.bitwise_and)
    ts(col("ge"), col("pb"), 0.0, None, A.is_equal)
    ts(col("go"), col("pb"), 0.0, None, A.is_gt)
    fill(reg("thr", 0, 4 * MW), BIG)
    cp(col("ipf"), col("pm"))
    cp(col("pf"), col("pi"))
    fill(reg("prf", 0, 10), 0.0)
    for b in range(4):
        quant("qe", "se", 128 * b, 128 * b + 128, "ebuf", 4 - b, 516 - b)
    for k in "eo":
        act(reg("eb" + k, 0, 520), reg("ebuf", 0, 520), col("g" + k))
        for b in range(4):
            quant("qe" + k, "se" + k, 128 * b, 128 * b + 128, "eb" + k, 4 - b, 516 - b)
    D, E = reg("dd", 0, 4 * LC), reg("lo", 0, 4 * LC)
    relu(E, D, ACT.Abs, 1.0, -7.5)
    for t in range(4):
        w = MW * t
        relu(reg("thr", w, w + LC), reg("lo", LC * t, LC * t + LC), ACT.Relu, BIG2, -7.5 * BIG2)
        relu(reg("thr", w + LC + 2, w + 2 * LC + 2), reg("dd", LC * t, LC * t + LC), ACT.Relu, BIG2, BIG2)
    relu(col("thr", 2 * LC + 2), col("pf"), ACT.Relu, BIG2, 0.0)
    cp(reg("prf", 1, 9), reg("prow", 0, 8))
    ins("g", lambda: g.partition_broadcast(T.pall[:, :], T.prf[0:1, :], 128), [reg("prf", 0, 10)], [reg("pall", 0, 10)])
    sel(reg("pme", 0, 10), reg("pall", 0, 10), [[-32, 5], [0, 2]], A.is_ge, 0.0, 0, 1)
    sel(reg("pmo", 0, 8), reg("pall", 1, 9), [[-32, 4], [0, 2]], A.is_ge, 0.0, 0, 1)
    iota("jio", 2 * LC, [[0, 2], [16, LC]], 0, 0)
    quant("qu", "su", 0, 128, "ut", 0, 512)

    def late_constants():
        fill(reg("thr", 2 * LC + 3, 4 * MW, MW), 0.0)
        lo2 = GRP[1] + 128 - GRP[2]
        ins("v", lambda: g.vector.memset(T.thr[0:lo2, 2 * MW:3 * MW], BIG), [], [reg("thr", 2 * MW, 3 * MW)])
        fill(reg("mt", 0, 4 * NM), 0.0)
        ts(reg("ltri", 0, 512), reg("lio", 0, 512), col("ipf"), None, A.is_ge)
        quant("ql", "sl", 0, 128, "ltri", 0, 512)
        quant("ql", "sl", 128, 256, "ones", 0, 512)
        ts(reg("jt", 0, 2 * LC), reg("jio", 0, 2 * LC), col("ipf"), 64.25, A.add, A.add)
        ins("v", lambda: g.vector.tensor_reduce(T.pce[:, 0:1], T.pme[:, :], AxisListType.X, A.add), [reg("pme", 0, 10)], [col("pce")])
        ins("v", lambda: g.vector.tensor_reduce(T.pco[:, 0:1], T.pmo[:, :], AxisListType.X, A.add), [reg("pmo", 0, 8)], [col("pco")])
        for k in "eo":
            ts(col("pz" + k), col("pc" + k), -64.0, None, A.add)
            ts(col("nc%s0" % k), col("pc" + k), -1.0, -64.0, A.mult, A.add)

    def quant_x(t, a, b):
        quant("qx%d" % t, "sx%d" % t, a, b, "xt", 4 * a, 4 * b)

    dst = T.cores[(rank - 1) % len(T.cores)]
    rid, pid = topo.addr(dst)[0:2]
    eng = topo.engines(core, dst)
    msk = sum(1 << e for e in eng[::len(eng) // NENG])

    def send(t):
        q, s = "qx%d" % t, "sx%d" % t
        for d in deps("g", [reg(q, 0, H), reg(s, 0, H)], []):
            await_("g", d)
        g.remote_dma(T[q][:, C:C + H].bitcast(dt.uint8), T[q][:, 0:H].bitcast(dt.uint8), T.sem["arr%d" % t], T.sem.loc, pid, rid, msk)
        g.remote_dma(T[s][:, C:C + H], T[s][:, 0:H], T.sem["arr%d" % t], T.sem.loc, pid, rid, msk)
        tot["loc"] = tot.get("loc", 0) + 2 * NENG
        tot["arr%d" % t] = 2 * NENG
        note("r", [], [reg(q, C, C + H), reg(s, C, C + H)], ("arr%d" % t, 2 * NENG, {}))

    def drive_mm(t, i):
        mm(i, "qx%d" % t, "sx%d" % t, GRP[i], "qu", "su", 0, 128)

    def flags(t, i):
        ts(reg("mt", i, 4 * MW, 4), reg("thr", MW * i, MW * i + MW), col("ps", 512 * i), None, A.is_lt)

    def near_mm(t, b, a, e):
        mm(b + (4 if a else 0), "qe", "se", 128 * b, "qx%d" % t, "sx%d" % t, a, e, True, False)

    NB = 7

    def count_mm(t):
        quant("qm%d" % t, "sm%d" % t, 0, NM, "mt", 0, 4 * NM)
        for b in range(NEARLY):
            near_mm(t, b, 0, C1)
        mm(NB, "ql", "sl", 0, "qm%d" % t, "sm%d" % t, 0, 128, True, False)
        mm(NB, "ql", "sl", 128, "qm%d" % t, "sm%d" % t, LC + 2, LC + 130, False, True)

    def chain(t):
        n = LC
        F = lambda nm: reg(nm, 0, n)
        N = bank(NB, n)
        hb = -127.0 / 256.0 if t == 0 else col("hb%d" % (t - 1))
        ts(F("hh"), N, STEP / 128.0, hb, A.mult, A.add)
        if t == 0:
            cp(col("fz"), col("ps", 512 * NB + LC))
        ts(F("vv"), F("hh"), 128.0 / STEP, None, A.mult)
        ts(F("rr"), F("hh"), 128.0 / STEP, col("fz"), A.mult, A.max)
        ts(F("par"), F("hh"), 1, None, A.bitwise_and)
        tt(F("nv"), N, F("vv"), A.subtract)
        tt(F("xx"), F("vv"), F("rr"), A.subtract)
        tt(F("nx"), F("rr"), F("vv"), A.subtract)
        ts(F("sg"), F("par"), 2.0, -1.0, A.mult, A.add)
        tt(F("z1"), F("xx"), F("nx"), A.max)
        for k in "eo":
            ts(F("t2" + k), F("nv"), float(STEP), col("nc%s%d" % (k, t)), A.mult, A.add)
        for k in "eo":
            ts(F("t1" + k), F("z1"), float(STEP), col("pz" + k), A.mult, A.add)
        for k in "eo":
            tt(F("yy" + k), F("t1" + k), F("t2" + k), A.max)
        for i, k in enumerate("eo"):
            tt(reg("sy", n * i, n * i + n), F("yy" + k), F("sg"), A.mult)
        tt(reg("of", 0, 2 * n), reg("sy", 0, 2 * n), reg("jt", 0, 2 * n), A.add)
        cp(reg("off%d" % t, 0, 2 * n), reg("of", 0, 2 * n))

    def carry(t):
        tl = col("ps", 512 * NB + LC + 1)
        if t == 0:
            cp(col("base0"), tl)
        else:
            tt(col("base%d" % t), tl, col("base%d" % (t - 1)), A.add)

    def carry2(t):
        ts(col("hb%d" % t), col("base%d" % t), STEP / 128.0, -127.0 / 256.0, A.mult, A.add)
        for k in "eo":
            ts(col("nc%s%d" % (k, t + 1)), col("base%d" % t), float(STEP), col("nc%s0" % k), A.mult, A.add)

    def pick(t, k, a, e, win):
        i = 0 if k == "e" else LC
        l = reg("off%d" % t, i + a // 16, i + e // 16)
        q, s, qw, sw = "qf%s%d" % (k, t), "sf%s%d" % (k, t), "qx%d" % t, "sx%d" % t
        ins("v", lambda: g.vector.tensor_copy(T[q][:, a:e].bitcast(dt.uint32), T[qw][:, 0:win].bitcast(dt.uint32).indirect(ap(l))), [reg(qw, 0, win), l], [reg(q, a, e)])
        ins("s", lambda: g.scalar.activation(T[s][:, a:e], T[sw][:, 0:win].indirect(ap(l)), ACT.Copy), [reg(sw, 0, win), l], [reg(s, a, e)])

    def far_mm(t, k, b, a, e):
        mm(b + (4 if a else 0), "qe" + k, "se" + k, 128 * b, "qf%s%d" % (k, t), "sf%s%d" % (k, t), a, e, False, k == "o")

    def blend(b, a, e, q):
        o, i = reg("zt", 4 * a + b, 4 * e, 4), bank(b + (4 if a else 0), e - a)
        if q == "s":
            act(o, i, 0.5)
        else:
            ts(o, i, 0.5, None, A.mult)

    def quant_z(t, a, e):
        quant("qz%d" % t, "sz%d" % t, a, e, "zt", 4 * a, 4 * e)

    def layer(t, b, a, e):
        mm(b + (4 if a else 0), "qw", "sw", 128 * b, "qz%d" % t, "sz%d" % t, a, e)

    def grow(b, a, e):
        y = reg("yt", 4 * a + b, 4 * e, 4)
        tt(y, bank(b + (4 if a else 0), e - a), y, A.add)

    quant_x(0, 0, P0)
    send(0)
    iota("atab", 128, [[1, 128]], 0, 0)
    late_constants()
    quant_x(0, P0, P1)
    act(reg("yt", 0, 4 * P1), reg("xt", 0, 4 * P1), 32.0)
    quant_x(0, P1, C)
    act(reg("yt", 4 * P1, 4 * C), reg("xt", 4 * P1, 4 * C), 32.0)
    for i in range(4):
        drive_mm(0, i)
    for i in range(4):
        flags(0, i)
    for t in range(R):
        last = t == R - 1
        count_mm(t)
        for b in range(NEARLY, 4):
            near_mm(t, b, 0, C1)
        chain(t)
        if not last:
            carry(t)
        for b in range(4):
            near_mm(t, b, C1, C)
        pick(t, "e", 0, C1, C)
        for b in range(4):
            far_mm(t, "e", b, 0, C1)
        pick(t, "o", 0, C1, C)
        for b in range(4):
            far_mm(t, "o", b, 0, C1)
        for k in "eo":
            pick(t, k, C1, C, C + H)
        for k in "eo":
            for b in range(4):
                far_mm(t, k, b, C1, C)
        if not last:
            carry2(t)
        else:
            F = lambda nm: reg(nm, 0, LC)
            ts(F("a1"), reg("sy", 0, LC), col("ge"), 64.25, A.mult, A.add)
            ts(F("a2"), reg("sy", LC, 2 * LC), col("go"), None, A.mult)
            tt(F("a3"), F("a1"), F("a2"), A.add)
            cp(F("aoff"), F("a3"))
            quant("qv", "sv", 0, 128, "vt", 0, 512)
        for b in range(4):
            blend(b, 0, C1, CAST1[b])
        quant_z(t, 0, C1)
        for b in range(4):
            layer(t, b, 0, C1)
        for b in range(4):
            blend(b, C1, C, CAST2[b])

        def grow1(b):
            grow(b, 0, C1)
            act(reg("xt", b, 4 * C1, 4), reg("yt", b, 4 * C1, 4), 0.03125)
        for b in range(ZAT):
            grow1(b)
        quant_z(t, C1, C)
        for b in range(4):
            layer(t, b, C1, C)
        for b in range(ZAT, 4):
            grow1(b)
        for b in range(4):
            grow(b, C1, C)
        ts(reg("xt", 4 * C1, 4 * C), reg("yt", 4 * C1, 4 * C), 0.03125, None, A.mult)
        n = t + 1
        if not last:
            quant_x(n, 0, P0)
            send(n)
            quant_x(n, P0, C1)
            early = sum(1 for k in GRP if k + 128 <= C1)
            for i in range(early):
                drive_mm(n, i)
            quant_x(n, C1, C)
            for i in range(early, 4):
                drive_mm(n, i)
            for i in range(4):
                flags(n, i)
        else:
            q, s = "qx%d" % n, "sx%d" % n
            w, l, o = reg("atab", 0, 128), reg("aoff", 0, LC), reg("ag", 0, C)
            ins("s", lambda: g.scalar.activation(ap(o), ap(w).indirect(ap(l)), ACT.Copy), [w, l], [o])
            dma("y", T.ao[:, :], T.ag[0:128:16, :], [o], [])
            quant_x(n, 0, C1)
            mm(0, "qv", "sv", 0, q, s, 0, C1)
            dma("y", T.oc[:, 0:4 * C1], T[q][:, 0:C1].bitcast(dt.uint8), [reg(q, 0, C1)], [])
            quant_x(n, C1, C)
            mm(1, "qv", "sv", 0, q, s, C1, C)
            act(reg("yo", 0, C1), bank(0, C1))
            cp(reg("yo", C1, C), bank(1, C - C1))
            dma("y", T.oc[:, 4 * C1:4 * C], T[q][:, C1:C].bitcast(dt.uint8), [reg(q, C1, C)], [])
            for k in range(4):
                dma("s" if k > 1 else "y", T.osc[4 * k:4 * k + 4, :], T[s][32 * k:32 * k + 4, 0:C], [reg(s, 0, C)], [])
            dma("y", T.y[:, :], T.yo[:, :], [reg("yo", 0, C)], [])
    for sem, n in tot.items():
        if know["g"].get(sem, 0) < n:
            g.wait_ge(T.sem[sem], n)
